import numpy as np
import ml_dtypes


def mxq(x, axis, fmt="e4m3"):
    dtype, down = {"e4m3": (ml_dtypes.float8_e4m3fn, 7), "e5m2": (ml_dtypes.float8_e5m2, 14)}[fmt]
    v = np.moveaxis(np.asarray(x, np.float32).astype(ml_dtypes.bfloat16).astype(np.float64), axis, -1)
    blocks = v.reshape(v.shape[:-1] + (-1, 32))
    amax = np.abs(blocks).max(-1, keepdims=True)
    byte = np.maximum(np.where(amax > 0, np.frexp(amax)[1] - 1 + 127, 0) - down, 1)
    scale = np.exp2(byte - 127.0)
    codes = (blocks / scale).astype(np.float32).astype(dtype).astype(np.float64)
    return np.moveaxis((codes * scale).reshape(v.shape), -1, axis)


WIDE = False


def mx_kscale(k):
    if not WIDE:
        return np.ones(k)
    levels = np.array([10, -10, 5, -5, 0])
    if k % 512:
        return np.exp2(np.random.permutation(np.resize(levels, k // 32))).repeat(32)
    a = np.empty((k // 512, 16))
    for p in range(k // 512):
        a[p, :8] = np.random.permutation(np.resize(levels, 8))
        for g in range(8):
            far = levels[np.abs(levels - a[p, g]) >= 10]
            a[p, g + 8] = far[np.random.randint(len(far))]
    return np.exp2(a.ravel()).repeat(32)


def f64(x):
    return np.asarray(x).astype(np.float64)


def striped(idx):
    return np.tile(np.asarray(idx).reshape(-1, 16).T, (8, 1)).astype(np.uint16)


def unstriped(offs):
    return offs[:16].T.reshape(-1).astype(np.int64)


E2M1 = np.array([0.0, 0.5, 1.0, 1.5, 2.0, 3.0, 4.0, 6.0, -0.0, -0.5, -1.0, -1.5, -2.0, -3.0, -4.0, -6.0])


def pack_weight(w, fmt):
    k, n = w.shape
    w = f64(np.asarray(w, np.float32).astype(ml_dtypes.bfloat16)).reshape(k // 32, 32, n)
    amax = np.abs(w).max(1)
    if fmt == "e4m3":
        byte = np.frexp(amax)[1] - 1 + 127 - 7
    else:
        mant, ex = np.frexp(amax / 6.0)
        byte = np.where(mant > 0.5, ex, ex - 1) + 127
    byte = np.clip(np.where(amax > 0, byte, 1), 1, 254)
    scaled = (w * np.exp2(127.0 - byte)[:, None, :]).reshape(k, n).astype(np.float32)
    by_word = np.ascontiguousarray(scaled.reshape(k // 512, 128, 4, n).transpose(0, 1, 3, 2))
    if fmt == "e4m3":
        words = by_word.astype(ml_dtypes.float8_e4m3fn).view(np.uint8)
    else:
        c = by_word.astype(ml_dtypes.float4_e2m1fn).view(np.uint8) & 0xF
        words = (c[..., 0::2] | (c[..., 1::2] << 4)).reshape(k // 512, 128, 2 * n)
    return np.ascontiguousarray(words), np.ascontiguousarray(byte.astype(np.uint8).reshape(k // 512, 16, n))


def unpack_weight(words, scales, fmt):
    g, _, n = scales.shape
    words = np.ascontiguousarray(words).reshape(g, 128, n, -1)
    if fmt == "e4m3":
        vals = words.view(ml_dtypes.float8_e4m3fn).astype(np.float64)
    else:
        nib = np.empty((g, 128, n, 4), np.uint8)
        nib[..., 0::2] = words & 0xF
        nib[..., 1::2] = words >> 4
        vals = E2M1[nib]
    vals = vals * np.repeat(np.exp2(scales.astype(np.float64) - 127.0), 8, axis=1)[..., None]
    return vals.transpose(0, 1, 3, 2).reshape(g * 512, n)


def bf(x):
    return np.asarray(x, np.float32).astype(ml_dtypes.bfloat16)


def planes(Y):
    r, m = Y.shape
    b = f64(bf(Y)).reshape(r // 32, 32, m)
    amax = np.abs(b).max(1)
    byte = np.clip(np.where(amax > 0, np.frexp(amax)[1] - 1 + 127 - 7, 1), 1, 254)
    codes = (b * np.exp2(127.0 - byte)[:, None, :]).reshape(r, m).astype(np.float32).astype(ml_dtypes.float8_e4m3fn).view(np.uint8)
    words = codes.reshape(r // 512, 128, 4, m).transpose(0, 1, 3, 2)
    return np.ascontiguousarray(words), np.ascontiguousarray(byte.astype(np.uint8).reshape(r // 512, 16, m))


D, T, I, Q, E, U = 512, 1024, 512, 256, 512, 256


def setup_inputs():
    n = np.random.standard_normal
    idx = np.random.permutation(T)[:I]
    idx2 = np.random.randint(0, U, I)
    fd = mx_kscale(D)
    fi = mx_kscale(I)
    keysp = pack_weight(n((D, T)) / fd[:, None], "e2m1")
    return {
        "query": (n((D, Q)) * 0.25 / np.sqrt(D) * fd[:, None]).astype(np.float32),
        "keys_words": keysp[0],
        "keys_scales": keysp[1],
        "size": (np.random.uniform(0.5, 2.0, (1, I)) * fi).astype(np.float32),
        "vals": (n((E, T))).astype(np.float32),
        "low": (np.random.uniform(-1.5, -0.3, (E, U))).astype(np.float32),
        "high": (np.random.uniform(0.3, 1.5, (E, U))).astype(np.float32),
        "vsc": (np.random.uniform(0.5, 2.0, (I, 1)) / fi[:, None]).astype(np.float32),
        "offs": striped(idx),
        "offs2": striped(idx2),
    }


def reference(query, keys_words, keys_scales, size, vals, low, high, vsc, offs, offs2):
    idx = unstriped(offs)
    idx2 = unstriped(offs2)
    keysu = unpack_weight(keys_words, keys_scales, "e2m1")
    queryq = mxq(f64(query), 0, "e4m3")
    keysidxg = keysu[:, idx]
    a = queryq.T @ keysidxg
    p = np.exp(a - np.max(a, axis=1, keepdims=True))
    w = p * f64(size) / np.sum(p, axis=1, keepdims=True)
    wt = w.T
    vb = np.minimum(np.maximum(f64(vals)[:, idx], f64(low)[:, idx2]), f64(high)[:, idx2])
    vt = vb.T
    vv = vt * f64(vsc)
    vvq = mxq(vv, 0, "e4m3")
    wtq = mxq(wt, 0, "e4m3")
    o = vvq.T @ wtq
    words, scales = planes(o)
    return o, words, scales

@@ -1,0 +1,203 @@
+from contextlib import ExitStack
+
+import concourse.mybir as mybir
+from concourse.masks import make_identity
+
+F32 = mybir.dt.float32
+BF16 = mybir.dt.bfloat16
+I32 = mybir.dt.int32
+U32 = mybir.dt.uint32
+U16 = mybir.dt.uint16
+U8 = mybir.dt.uint8
+FP8X4 = mybir.dt.float8_e4m3fn_x4
+FP4X4 = mybir.dt.float4_e2m1fn_x4
+ALU = mybir.AluOpType
+ACT = mybir.ActivationFunctionType
+AXIS_X = mybir.AxisListType.X
+
+D, T, I, Q, E, U = 512, 1024, 512, 256, 512, 256
+P = 128
+PACK = 4
+RUN = 8
+WINDOW = 704
+FLOPS = 2 * D * Q * I + 2 * I * E * Q
+
+
+def tile_attend_boundedvalues_pl_kernel(
+    tc, query, keys_words, keys_scales, size, vals, low, high, vsc, offs, offs2, out_0, out_1, out_2
+):
+    nc = tc.nc
+    halves = Q // P
+    with ExitStack() as ctx:
+        sb = ctx.enter_context(tc.tile_pool(name="sb", bufs=1))
+        ps = ctx.enter_context(tc.psum_pool(name="ps", bufs=1))
+
+        def tile(shape, dtype, name):
+            return sb.tile(shape, dtype, name=name, align_bytes=64)
+
+        slots = tile([P, I // 16], U16, "slots")
+        classes = tile([P, I // 16], U16, "classes")
+        kwords = tile([P, T], U16, "kwords")
+        kbytes = tile([P, T], U8, "kbytes")
+        table_w = (PACK - 1) * U + WINDOW
+        low_sb = tile([P, table_w], F32, "low_sb")
+        high_sb = tile([P, table_w], F32, "high_sb")
+        vals_sb = [tile([P, T], F32, "vals%d" % j) for j in range(PACK)]
+        q_raw = tile([P, PACK, Q], F32, "q_raw")
+        rows = tile([P, P], F32, "rows")
+        ident = tile([P, P], F32, "ident")
+
+        nc.vector.memset(kbytes[:].bitcast(I32), 0)
+        nc.vector.memset(low_sb[:, PACK * U :], 0.0)
+        nc.vector.memset(high_sb[:, PACK * U :], 0.0)
+        nc.gpsimd.memset(rows[:], 0.0)
+        make_identity(nc, ident[:])
+
+        vals_v = vals.rearrange("(p j) t -> j p t", j=PACK)
+        nc.sync.dma_start(slots[:], offs)
+        nc.sync.dma_start(kwords[:].bitcast(I32), keys_words[0].bitcast(I32))
+        nc.sync.dma_start(classes[:], offs2)
+        nc.sync.dma_start(low_sb[:, : PACK * U], low.rearrange("(p j) u -> p (j u)", j=PACK))
+        nc.sync.dma_start(vals_sb[0][:], vals_v[0])
+        nc.sync.dma_start(high_sb[:, : PACK * U], high.rearrange("(p j) u -> p (j u)", j=PACK))
+        nc.sync.dma_start(q_raw[:], query.rearrange("(p j) q -> p j q", j=PACK))
+        for g in range(4):
+            nc.sync.dma_start(
+                kbytes[32 * g : 32 * g + 4, :].bitcast(I32), keys_scales[0, 4 * g : 4 * g + 4, :].bitcast(I32)
+            )
+        nc.sync.dma_start(
+            rows[0:PACK, :].rearrange("t (b r) -> t b r", r=RUN),
+            vsc.rearrange("(b t r) o -> t b (r o)", t=PACK, r=RUN),
+        )
+        nc.sync.dma_start(
+            rows[PACK : 2 * PACK, :].rearrange("t (b r) -> t b r", r=RUN),
+            size.rearrange("o (b t r) -> (o t) b r", t=PACK, r=RUN),
+        )
+        for j in range(1, PACK):
+            nc.sync.dma_start(vals_sb[j][:], vals_v[j])
+
+        kg_words = tile([P, I], U16, "kg_words")
+        kg_bytes = tile([P, I], U8, "kg_bytes")
+        nc.vector.tensor_copy(kg_words[:], kwords[:].indirect(slots[:]))
+        nc.vector.tensor_copy(kg_bytes[:], kbytes[:].indirect(slots[:]))
+
+        turned = ps.tile([P, PACK, P], F32, name="turned", tag="turn", bufs=2)
+        nc.tensor.transpose(turned[:, 0, :], rows[:], ident[:])
+        cols = tile([P, 2 * PACK], F32, "cols")
+        nc.scalar.copy(cols[:], turned[:, 0, : 2 * PACK])
+
+        q_bf = tile([P, Q, PACK], BF16, "q_bf")
+        nc.scalar.copy(
+            q_bf[:].rearrange("p (c i) t -> p c t i", i=4), q_raw[:].rearrange("p t (c i) -> p c t i", i=4)
+        )
+        q_words = tile([P, Q], U32, "q_words")
+        q_bytes = tile([P, Q], U8, "q_bytes")
+        nc.vector.quantize_mx(q_words[:].bitcast(FP8X4), q_bytes[:], q_bf[:].rearrange("p q t -> p (q t)"))
+
+        neg_max = tile([P, halves], F32, "neg_max")
+        sums = tile([P, halves], F32, "sums")
+        inv = tile([P, halves], F32, "inv")
+        probs = []
+        for h in range(halves):
+            cs = slice(h * P, (h + 1) * P)
+            score = ps.tile([P, I], F32, name="score%d" % h)
+            nc.tensor.matmul_mx(
+                score[:], lhsT=q_words[:, cs].bitcast(FP8X4), lhsT_scale=q_bytes[:, cs],
+                rhs=kg_words[:].bitcast(FP4X4), rhs_scale=kg_bytes[:], start=True, stop=True,
+            )
+            nc.vector.tensor_reduce(neg_max[:, h : h + 1], score[:], AXIS_X, ALU.max, negate=True)
+            prob = tile([P, PACK, P], F32, "prob%d" % h)
+            nc.scalar.activation(
+                prob[:].rearrange("p t (b r) -> p t b r", r=RUN),
+                score[:].rearrange("p (b t r) -> p t b r", t=PACK, r=RUN),
+                ACT.Exp, bias=neg_max[:, h : h + 1], scale=1.0, accum_out=sums[:, h : h + 1],
+            )
+            probs.append(prob)
+        nc.vector.reciprocal(inv[:], sums[:])
+        w_banks = [ps.tile([P, 2, Q], F32, name="w_bank%d" % u) for u in range(2)]
+        for h in range(halves):
+            norm = tile([P, PACK, P], F32, "norm%d" % h)
+            nc.scalar.activation(norm[:], probs[h][:], ACT.Copy, scale=inv[:, h : h + 1])
+            for t in range(PACK):
+                nc.tensor.transpose(w_banks[t // 2][:, t % 2, h * P : (h + 1) * P], norm[:, t, :], ident[:])
+        w_planes = tile([P, PACK, Q], BF16, "w_planes")
+        for t in range(PACK):
+            nc.scalar.activation(
+                w_planes[:, t, :], w_banks[t // 2][:, t % 2, :], ACT.Copy, scale=cols[:, PACK + t : PACK + t + 1]
+            )
+        w_bf = tile([P, Q, PACK], BF16, "w_bf")
+        nc.scalar.copy(
+            w_bf[:].rearrange("p (c i) t -> p c t i", i=4), w_planes[:].rearrange("p t (c i) -> p c t i", i=4)
+        )
+        w_words = tile([P, Q], U32, "w_words")
+        w_bytes = tile([P, Q], U8, "w_bytes")
+        nc.vector.quantize_mx(w_words[:].bitcast(FP8X4), w_bytes[:], w_bf[:].rearrange("p q t -> p (q t)"))
+
+        out_banks = [ps.tile([P, PACK, P], F32, name="out_bank%d" % h) for h in range(halves)]
+        y = tile([P, PACK, Q], F32, "y")
+        out_v = out_0.rearrange("(p t) q -> p t q", t=PACK)
+
+        for j in range(PACK):
+            lo = sb.tile([P, I], F32, name="lo", tag="lo", bufs=2, align_bytes=64)
+            hi = sb.tile([P, I], F32, name="hi", tag="hi", bufs=2, align_bytes=64)
+            val = tile([P, I], F32, "val%d" % j)
+            nc.vector.tensor_copy(lo[:], low_sb[:, j * U : j * U + WINDOW].indirect(classes[:]))
+            nc.vector.tensor_copy(val[:], vals_sb[j][:].indirect(slots[:]))
+            nc.vector.tensor_copy(hi[:], high_sb[:, j * U : j * U + WINDOW].indirect(classes[:]))
+            floor = tile([P, I], F32, "floor%d" % j)
+            nc.vector.tensor_tensor(floor[:], val[:], lo[:], ALU.max)
+            cut = tile([P, PACK, P], F32, "cut%d" % j)
+            nc.vector.tensor_tensor(
+                cut[:].rearrange("p t (b r) -> p t b r", r=RUN),
+                floor[:].rearrange("p (b t r) -> p t b r", t=PACK, r=RUN),
+                hi[:].rearrange("p (b t r) -> p t b r", t=PACK, r=RUN),
+                ALU.min,
+            )
+            bank = ps.tile([P, PACK, P], F32, name="turned", tag="turn", bufs=2)
+            for t in range(PACK):
+                nc.tensor.transpose(bank[:, t, :], cut[:, t, :], ident[:])
+            v_bf = tile([P, P, PACK], BF16, "v_bf%d" % j)
+            if j < PACK - 1:
+                v_planes = tile([P, PACK, P], BF16, "v_planes%d" % j)
+                for t in range(PACK):
+                    nc.scalar.activation(v_planes[:, t, :], bank[:, t, :], ACT.Copy, scale=cols[:, t : t + 1])
+                nc.scalar.copy(
+                    v_bf[:].rearrange("p (c i) t -> p c t i", i=4),
+                    v_planes[:].rearrange("p t (c i) -> p c t i", i=4),
+                )
+            else:
+                nc.vector.tensor_tensor(
+                    v_bf[:], bank[:].rearrange("p t e -> p e t"),
+                    cols[:, 0:PACK].unsqueeze(1).to_broadcast([P, P, PACK]), ALU.mult,
+                )
+            v_words = tile([P, P], U32, "v_words%d" % j)
+            v_bytes = tile([P, P], U8, "v_bytes%d" % j)
+            nc.vector.quantize_mx(v_words[:].bitcast(FP8X4), v_bytes[:], v_bf[:].rearrange("p e t -> p (e t)"))
+            for h in range(halves):
+                cs = slice(h * P, (h + 1) * P)
+                nc.tensor.matmul_mx(
+                    out_banks[h][:, j, :], lhsT=v_words[:].bitcast(FP8X4), lhsT_scale=v_bytes[:],
+                    rhs=w_words[:, cs].bitcast(FP8X4), rhs_scale=w_bytes[:, cs], start=True, stop=True,
+                )
+            if j == 1:
+                for h in range(halves):
+                    nc.scalar.copy(y[:, 0:2, h * P : (h + 1) * P], out_banks[h][:, 0:2, :])
+                nc.sync.dma_start(out_v[:, 0:2, :], y[:, 0:2, :])
+
+        y_bf = [tile([P, P, PACK], BF16, "y_bf%d" % h) for h in range(halves)]
+        nc.vector.tensor_copy(y_bf[0][:], out_banks[0][:].rearrange("p t q -> p q t"))
+        nc.scalar.copy(y_bf[1][:], out_banks[1][:].rearrange("p t q -> p q t"))
+        for h in (1, 0):
+            nc.scalar.copy(y[:, 2:4, h * P : (h + 1) * P], out_banks[h][:, 2:4, :])
+        y_words = tile([P, Q], U32, "y_words")
+        y_bytes = tile([P, Q], U8, "y_bytes")
+        for h in range(halves):
+            cs = slice(h * P, (h + 1) * P)
+            nc.vector.quantize_mx(
+                y_words[:, cs].bitcast(FP8X4), y_bytes[:, cs], y_bf[h][:].rearrange("p q t -> p (q t)")
+            )
+        nc.scalar.dma_start(out_v[:, 2:4, :], y[:, 2:4, :])
+        nc.sync.dma_start(out_1[0].rearrange("p q t -> p (q t)").bitcast(I32), y_words[:].bitcast(I32))
+        for g in range(4):
+            queue = nc.sync if g < 2 else nc.scalar
+            queue.dma_start(out_2[0, 4 * g : 4 * g + 4, :].bitcast(I32), y_bytes[32 * g : 32 * g + 4, :].bitcast(I32))

@@ -35,36 +35,46 @@ def tile_attend_boundedvalues_pl_kernel(
         def tile(shape, dtype, name):
             return sb.tile(shape, dtype, name=name, align_bytes=64)
 
+        def after(tag, shape, dtype, name):
+            return sb.tile(shape, dtype, name=name, tag=tag, bufs=1, align_bytes=64)
+
+        def dealt(ap):
+            return ap[:].rearrange("p (b t r) -> p t b r", t=PACK, r=RUN)
+
         slots = tile([P, I // 16], U16, "slots")
         classes = tile([P, I // 16], U16, "classes")
         kwords = tile([P, T], U16, "kwords")
         kbytes = tile([P, T], U8, "kbytes")
         table_w = (PACK - 1) * U + WINDOW
-        low_sb = tile([P, table_w], F32, "low_sb")
+        low_first = tile([P, WINDOW], F32, "low_first")
+        low_sb = tile([P, table_w - U], F32, "low_sb")
         high_sb = tile([P, table_w], F32, "high_sb")
         vals_sb = [tile([P, T], F32, "vals%d" % j) for j in range(PACK)]
-        q_raw = tile([P, PACK, Q], F32, "q_raw")
+        q_raw = after("lo2", [P, PACK, Q], F32, "q_raw")
         rows = tile([P, P], F32, "rows")
         ident = tile([P, P], F32, "ident")
 
-        nc.vector.memset(kbytes[:].bitcast(I32), 0)
-        nc.vector.memset(low_sb[:, PACK * U :], 0.0)
+        nc.gpsimd.memset(kbytes[:].bitcast(I32), 0)
+        nc.vector.memset(low_first[:, U:], 0.0)
+        nc.vector.memset(low_sb[:, (PACK - 1) * U :], 0.0)
         nc.vector.memset(high_sb[:, PACK * U :], 0.0)
         nc.gpsimd.memset(rows[:], 0.0)
         make_identity(nc, ident[:])
 
         vals_v = vals.rearrange("(p j) t -> j p t", j=PACK)
+        low_v = low.rearrange("(p j) u -> p (j u)", j=PACK)
+        nc.scalar.dma_start(low_first[:, :U], low_v[:, :U])
+        nc.sync.dma_start(classes[:], offs2)
         nc.sync.dma_start(slots[:], offs)
         nc.sync.dma_start(kwords[:].bitcast(I32), keys_words[0].bitcast(I32))
-        nc.sync.dma_start(classes[:], offs2)
-        nc.sync.dma_start(low_sb[:, : PACK * U], low.rearrange("(p j) u -> p (j u)", j=PACK))
-        nc.sync.dma_start(vals_sb[0][:], vals_v[0])
-        nc.sync.dma_start(high_sb[:, : PACK * U], high.rearrange("(p j) u -> p (j u)", j=PACK))
-        nc.sync.dma_start(q_raw[:], query.rearrange("(p j) q -> p j q", j=PACK))
+        nc.sync.dma_start(low_sb[:, : (PACK - 1) * U], low_v[:, U:])
         for g in range(4):
             nc.sync.dma_start(
                 kbytes[32 * g : 32 * g + 4, :].bitcast(I32), keys_scales[0, 4 * g : 4 * g + 4, :].bitcast(I32)
             )
+        nc.sync.dma_start(q_raw[:], query.rearrange("(p j) q -> p j q", j=PACK))
+        nc.sync.dma_start(vals_sb[0][:], vals_v[0])
+        nc.sync.dma_start(high_sb[:, : PACK * U], high.rearrange("(p j) u -> p (j u)", j=PACK))
         nc.sync.dma_start(
             rows[0:PACK, :].rearrange("t (b r) -> t b r", r=RUN),
             vsc.rearrange("(b t r) o -> t b (r o)", t=PACK, r=RUN),
@@ -81,7 +91,7 @@ def tile_attend_boundedvalues_pl_kernel(
         nc.vector.tensor_copy(kg_words[:], kwords[:].indirect(slots[:]))
         nc.vector.tensor_copy(kg_bytes[:], kbytes[:].indirect(slots[:]))
 
-        turned = ps.tile([P, PACK, P], F32, name="turned", tag="turn", bufs=2)
+        turned = ps.tile([P, PACK, P], F32, name="turned")
         nc.tensor.transpose(turned[:, 0, :], rows[:], ident[:])
         cols = tile([P, 2 * PACK], F32, "cols")
         nc.scalar.copy(cols[:], turned[:, 0, : 2 * PACK])
@@ -90,17 +100,17 @@ def tile_attend_boundedvalues_pl_kernel(
         nc.scalar.copy(
             q_bf[:].rearrange("p (c i) t -> p c t i", i=4), q_raw[:].rearrange("p t (c i) -> p c t i", i=4)
         )
-        q_words = tile([P, Q], U32, "q_words")
+        q_words = after("hi_even", [P, Q], U32, "q_words")
         q_bytes = tile([P, Q], U8, "q_bytes")
         nc.vector.quantize_mx(q_words[:].bitcast(FP8X4), q_bytes[:], q_bf[:].rearrange("p q t -> p (q t)"))
 
-        neg_max = tile([P, halves], F32, "neg_max")
-        sums = tile([P, halves], F32, "sums")
+        neg_max = after("val", [P, halves], F32, "neg_max")
+        sums = after("hi_odd", [P, halves], F32, "sums")
         inv = tile([P, halves], F32, "inv")
         probs = []
         for h in range(halves):
             cs = slice(h * P, (h + 1) * P)
-            score = ps.tile([P, I], F32, name="score%d" % h)
+            score = ps.tile([P, I], F32, name="score%d" % h, tag="pair%d" % h)
             nc.tensor.matmul_mx(
                 score[:], lhsT=q_words[:, cs].bitcast(FP8X4), lhsT_scale=q_bytes[:, cs],
                 rhs=kg_words[:].bitcast(FP4X4), rhs_scale=kg_bytes[:], start=True, stop=True,
@@ -120,7 +130,7 @@ def tile_attend_boundedvalues_pl_kernel(
             nc.scalar.activation(norm[:], probs[h][:], ACT.Copy, scale=inv[:, h : h + 1])
             for t in range(PACK):
                 nc.tensor.transpose(w_banks[t // 2][:, t % 2, h * P : (h + 1) * P], norm[:, t, :], ident[:])
-        w_planes = tile([P, PACK, Q], BF16, "w_planes")
+        w_planes = after("floor2", [P, PACK, Q], BF16, "w_planes")
         for t in range(PACK):
             nc.scalar.activation(
                 w_planes[:, t, :], w_banks[t // 2][:, t % 2, :], ACT.Copy, scale=cols[:, PACK + t : PACK + t + 1]
@@ -138,66 +148,91 @@ def tile_attend_boundedvalues_pl_kernel(
         out_v = out_0.rearrange("(p t) q -> p t q", t=PACK)
 
         for j in range(PACK):
-            lo = sb.tile([P, I], F32, name="lo", tag="lo", bufs=2, align_bytes=64)
-            hi = sb.tile([P, I], F32, name="hi", tag="hi", bufs=2, align_bytes=64)
-            val = tile([P, I], F32, "val%d" % j)
-            nc.vector.tensor_copy(lo[:], low_sb[:, j * U : j * U + WINDOW].indirect(classes[:]))
+            lo = after("lo%d" % min(j, 2), [P, I], F32, "lo%d" % j)
+            hi = after(("hi_even", "hi_odd")[j % 2], [P, I], F32, "hi%d" % j)
+            val = after("val", [P, I], F32, "val%d" % j)
+            low_window = low_first[:] if j == 0 else low_sb[:, (j - 1) * U : (j - 1) * U + WINDOW]
+            nc.vector.tensor_copy(lo[:], low_window.indirect(classes[:]))
             nc.vector.tensor_copy(val[:], vals_sb[j][:].indirect(slots[:]))
             nc.vector.tensor_copy(hi[:], high_sb[:, j * U : j * U + WINDOW].indirect(classes[:]))
-            floor = tile([P, I], F32, "floor%d" % j)
-            nc.vector.tensor_tensor(floor[:], val[:], lo[:], ALU.max)
+            floor = after("floor%d" % j, [P, I], F32, "floor%d" % j)
             cut = tile([P, PACK, P], F32, "cut%d" % j)
-            nc.vector.tensor_tensor(
-                cut[:].rearrange("p t (b r) -> p t b r", r=RUN),
-                floor[:].rearrange("p (b t r) -> p t b r", t=PACK, r=RUN),
-                hi[:].rearrange("p (b t r) -> p t b r", t=PACK, r=RUN),
-                ALU.min,
-            )
-            bank = ps.tile([P, PACK, P], F32, name="turned", tag="turn", bufs=2)
-            for t in range(PACK):
-                nc.tensor.transpose(bank[:, t, :], cut[:, t, :], ident[:])
+            for u in range(2):
+                nc.vector.tensor_tensor(
+                    floor[:, u * (I // 2) : (u + 1) * (I // 2)].rearrange("p (t b r) -> p t b r", t=2, r=RUN),
+                    dealt(val)[:, 2 * u : 2 * u + 2], dealt(lo)[:, 2 * u : 2 * u + 2], ALU.max,
+                )
+            step = 1 if j == PACK - 1 else 2
+            for t in range(0, PACK, step):
+                nc.vector.tensor_tensor(
+                    cut[:, t : t + step, :].rearrange("p t (b r) -> p t b r", r=RUN),
+                    floor[:, t * P : (t + step) * P].rearrange("p (t b r) -> p t b r", t=step, r=RUN),
+                    dealt(hi)[:, t : t + step], ALU.min,
+                )
             v_bf = tile([P, P, PACK], BF16, "v_bf%d" % j)
             if j < PACK - 1:
-                v_planes = tile([P, PACK, P], BF16, "v_planes%d" % j)
-                for t in range(PACK):
-                    nc.scalar.activation(v_planes[:, t, :], bank[:, t, :], ACT.Copy, scale=cols[:, t : t + 1])
+                v_planes = after("floor3" if j == 2 else "v_planes%d" % j, [P, PACK, P], BF16, "v_planes%d" % j)
+                for u in range(2):
+                    bank = ps.tile([P, 2, P], F32, name="pair%d_%d" % (j, u), tag="pair%d" % u)
+                    for t in range(2):
+                        nc.tensor.transpose(bank[:, t, :], cut[:, 2 * u + t, :], ident[:])
+                    for t in range(2):
+                        place = 2 * u + t
+                        nc.scalar.activation(
+                            v_planes[:, place, :], bank[:, t, :], ACT.Copy, scale=cols[:, place : place + 1]
+                        )
                 nc.scalar.copy(
                     v_bf[:].rearrange("p (c i) t -> p c t i", i=4),
                     v_planes[:].rearrange("p t (c i) -> p c t i", i=4),
                 )
             else:
-                nc.vector.tensor_tensor(
-                    v_bf[:], bank[:].rearrange("p t e -> p e t"),
-                    cols[:, 0:PACK].unsqueeze(1).to_broadcast([P, P, PACK]), ALU.mult,
-                )
+                bank = ps.tile([P, PACK, P], F32, name="last_bank")
+                for t in range(PACK):
+                    nc.tensor.transpose(bank[:, t, :], cut[:, t, :], ident[:])
+                for u in range(2):
+                    es = slice(u * (P // 2), (u + 1) * (P // 2))
+                    nc.vector.tensor_tensor(
+                        v_bf[:, es, :], bank[:, :, es].rearrange("p t e -> p e t"),
+                        cols[:, 0:PACK].unsqueeze(1).to_broadcast([P, P // 2, PACK]), ALU.mult,
+                    )
             v_words = tile([P, P], U32, "v_words%d" % j)
             v_bytes = tile([P, P], U8, "v_bytes%d" % j)
-            nc.vector.quantize_mx(v_words[:].bitcast(FP8X4), v_bytes[:], v_bf[:].rearrange("p e t -> p (e t)"))
+            pieces = 2 if j == PACK - 1 else 1
+            for u in range(pieces):
+                es = slice(u * (P // pieces), (u + 1) * (P // pieces))
+                nc.vector.quantize_mx(
+                    v_words[:, es].bitcast(FP8X4), v_bytes[:, es], v_bf[:, es, :].rearrange("p e t -> p (e t)")
+                )
             for h in range(halves):
                 cs = slice(h * P, (h + 1) * P)
                 nc.tensor.matmul_mx(
                     out_banks[h][:, j, :], lhsT=v_words[:].bitcast(FP8X4), lhsT_scale=v_bytes[:],
                     rhs=w_words[:, cs].bitcast(FP8X4), rhs_scale=w_bytes[:, cs], start=True, stop=True,
                 )
-            if j == 1:
+            if j == 2:
                 for h in range(halves):
-                    nc.scalar.copy(y[:, 0:2, h * P : (h + 1) * P], out_banks[h][:, 0:2, :])
-                nc.sync.dma_start(out_v[:, 0:2, :], y[:, 0:2, :])
+                    nc.scalar.copy(y[:, 0:3, h * P : (h + 1) * P], out_banks[h][:, 0:3, :])
+                nc.sync.dma_start(out_v[:, 0:3, :], y[:, 0:3, :])
 
         y_bf = [tile([P, P, PACK], BF16, "y_bf%d" % h) for h in range(halves)]
-        nc.vector.tensor_copy(y_bf[0][:], out_banks[0][:].rearrange("p t q -> p q t"))
+        for u in range(2):
+            qs = slice(u * (P // 2), (u + 1) * (P // 2))
+            nc.vector.tensor_copy(y_bf[0][:, qs, :], out_banks[0][:, :, qs].rearrange("p t q -> p q t"))
         nc.scalar.copy(y_bf[1][:], out_banks[1][:].rearrange("p t q -> p q t"))
         for h in (1, 0):
-            nc.scalar.copy(y[:, 2:4, h * P : (h + 1) * P], out_banks[h][:, 2:4, :])
+            nc.scalar.copy(y[:, 3, h * P : (h + 1) * P], out_banks[h][:, 3, :])
         y_words = tile([P, Q], U32, "y_words")
         y_bytes = tile([P, Q], U8, "y_bytes")
-        for h in range(halves):
-            cs = slice(h * P, (h + 1) * P)
+        for h, first, width in ((0, 0, P // 2), (0, P // 2, P // 2), (1, 0, P)):
+            cs = slice(h * P + first, h * P + first + width)
             nc.vector.quantize_mx(
-                y_words[:, cs].bitcast(FP8X4), y_bytes[:, cs], y_bf[h][:].rearrange("p q t -> p (q t)")
+                y_words[:, cs].bitcast(FP8X4), y_bytes[:, cs],
+                y_bf[h][:, first : first + width, :].rearrange("p q t -> p (q t)"),
             )
-        nc.scalar.dma_start(out_v[:, 2:4, :], y[:, 2:4, :])
-        nc.sync.dma_start(out_1[0].rearrange("p q t -> p (q t)").bitcast(I32), y_words[:].bitcast(I32))
+        nc.sync.dma_start(out_v[:, 3, :], y[:, 3, :])
+        words_v = out_1[0].rearrange("p q t -> p (q t)").bitcast(I32)
+        for h in range(halves):
+            nc.sync.dma_start(words_v[:, h * P : (h + 1) * P], y_words[:, h * P : (h + 1) * P].bitcast(I32))
         for g in range(4):
             queue = nc.sync if g < 2 else nc.scalar
             queue.dma_start(out_2[0, 4 * g : 4 * g + 4, :].bitcast(I32), y_bytes[32 * g : 32 * g + 4, :].bitcast(I32))

@@ -50,7 +50,7 @@ def tile_attend_boundedvalues_pl_kernel(
         low_sb = tile([P, table_w - U], F32, "low_sb")
         high_sb = tile([P, table_w], F32, "high_sb")
         vals_sb = [tile([P, T], F32, "vals%d" % j) for j in range(PACK)]
-        q_raw = after("lo2", [P, PACK, Q], F32, "q_raw")
+        q_raw = after("hi0", [P, PACK, Q], F32, "q_raw")
         rows = tile([P, P], F32, "rows")
         ident = tile([P, P], F32, "ident")
 
@@ -68,12 +68,11 @@ def tile_attend_boundedvalues_pl_kernel(
         nc.sync.dma_start(slots[:], offs)
         nc.sync.dma_start(kwords[:].bitcast(I32), keys_words[0].bitcast(I32))
         nc.sync.dma_start(low_sb[:, : (PACK - 1) * U], low_v[:, U:])
+        nc.sync.dma_start(q_raw[:], query.rearrange("(p j) q -> p j q", j=PACK))
         for g in range(4):
             nc.sync.dma_start(
                 kbytes[32 * g : 32 * g + 4, :].bitcast(I32), keys_scales[0, 4 * g : 4 * g + 4, :].bitcast(I32)
             )
-        nc.sync.dma_start(q_raw[:], query.rearrange("(p j) q -> p j q", j=PACK))
-        nc.sync.dma_start(vals_sb[0][:], vals_v[0])
         nc.sync.dma_start(high_sb[:, : PACK * U], high.rearrange("(p j) u -> p (j u)", j=PACK))
         nc.sync.dma_start(
             rows[0:PACK, :].rearrange("t (b r) -> t b r", r=RUN),
@@ -83,7 +82,7 @@ def tile_attend_boundedvalues_pl_kernel(
             rows[PACK : 2 * PACK, :].rearrange("t (b r) -> t b r", r=RUN),
             size.rearrange("o (b t r) -> (o t) b r", t=PACK, r=RUN),
         )
-        for j in range(1, PACK):
+        for j in range(PACK):
             nc.sync.dma_start(vals_sb[j][:], vals_v[j])
 
         kg_words = tile([P, I], U16, "kg_words")
@@ -100,12 +99,12 @@ def tile_attend_boundedvalues_pl_kernel(
         nc.scalar.copy(
             q_bf[:].rearrange("p (c i) t -> p c t i", i=4), q_raw[:].rearrange("p t (c i) -> p c t i", i=4)
         )
-        q_words = after("hi_even", [P, Q], U32, "q_words")
+        q_words = after("hi1", [P, Q], U32, "q_words")
         q_bytes = tile([P, Q], U8, "q_bytes")
         nc.vector.quantize_mx(q_words[:].bitcast(FP8X4), q_bytes[:], q_bf[:].rearrange("p q t -> p (q t)"))
 
         neg_max = after("val", [P, halves], F32, "neg_max")
-        sums = after("hi_odd", [P, halves], F32, "sums")
+        sums = after("hi2", [P, halves], F32, "sums")
         inv = tile([P, halves], F32, "inv")
         probs = []
         for h in range(halves):
@@ -149,7 +148,7 @@ def tile_attend_boundedvalues_pl_kernel(
 
         for j in range(PACK):
             lo = after("lo%d" % min(j, 2), [P, I], F32, "lo%d" % j)
-            hi = after(("hi_even", "hi_odd")[j % 2], [P, I], F32, "hi%d" % j)
+            hi = after("hi%d" % (j % 3), [P, I], F32, "hi%d" % j)
             val = after("val", [P, I], F32, "val%d" % j)
             low_window = low_first[:] if j == 0 else low_sb[:, (j - 1) * U : (j - 1) * U + WINDOW]
             nc.vector.tensor_copy(lo[:], low_window.indirect(classes[:]))

from contextlib import ExitStack

import concourse.mybir as mybir
from concourse.masks import make_identity

F32 = mybir.dt.float32
BF16 = mybir.dt.bfloat16
I32 = mybir.dt.int32
U32 = mybir.dt.uint32
U16 = mybir.dt.uint16
U8 = mybir.dt.uint8
FP8X4 = mybir.dt.float8_e4m3fn_x4
FP4X4 = mybir.dt.float4_e2m1fn_x4
ALU = mybir.AluOpType
ACT = mybir.ActivationFunctionType
AXIS_X = mybir.AxisListType.X

D, T, I, Q, E, U = 512, 1024, 512, 256, 512, 256
P = 128
PACK = 4
RUN = 8
WINDOW = 704
FLOPS = 2 * D * Q * I + 2 * I * E * Q


def tile_attend_boundedvalues_pl_kernel(
    tc, query, keys_words, keys_scales, size, vals, low, high, vsc, offs, offs2, out_0, out_1, out_2
):
    nc = tc.nc
    halves = Q // P
    with ExitStack() as ctx:
        sb = ctx.enter_context(tc.tile_pool(name="sb", bufs=1))
        ps = ctx.enter_context(tc.psum_pool(name="ps", bufs=1))

        def tile(shape, dtype, name):
            return sb.tile(shape, dtype, name=name, align_bytes=64)

        def after(tag, shape, dtype, name):
            return sb.tile(shape, dtype, name=name, tag=tag, bufs=1, align_bytes=64)

        def dealt(ap):
            return ap[:].rearrange("p (b t r) -> p t b r", t=PACK, r=RUN)

        slots = tile([P, I // 16], U16, "slots")
        classes = tile([P, I // 16], U16, "classes")
        kwords = tile([P, T], U16, "kwords")
        kbytes = tile([P, T], U8, "kbytes")
        table_w = (PACK - 1) * U + WINDOW
        low_first = tile([P, WINDOW], F32, "low_first")
        low_sb = tile([P, table_w - U], F32, "low_sb")
        high_sb = tile([P, table_w], F32, "high_sb")
        vals_sb = [tile([P, T], F32, "vals%d" % j) for j in range(PACK)]
        q_raw = after("hi0", [P, PACK, Q], F32, "q_raw")
        rows = tile([P, P], F32, "rows")
        ident = tile([P, P], F32, "ident")

        nc.gpsimd.memset(kbytes[:].bitcast(I32), 0)
        nc.vector.memset(low_first[:, U:], 0.0)
        nc.vector.memset(low_sb[:, (PACK - 1) * U :], 0.0)
        nc.vector.memset(high_sb[:, PACK * U :], 0.0)
        nc.gpsimd.memset(rows[:], 0.0)
        make_identity(nc, ident[:])

        vals_v = vals.rearrange("(p j) t -> j p t", j=PACK)
        low_v = low.rearrange("(p j) u -> p (j u)", j=PACK)
        nc.scalar.dma_start(low_first[:, :U], low_v[:, :U])
        nc.sync.dma_start(classes[:], offs2)
        nc.sync.dma_start(slots[:], offs)
        nc.sync.dma_start(kwords[:].bitcast(I32), keys_words[0].bitcast(I32))
        nc.sync.dma_start(low_sb[:, : (PACK - 1) * U], low_v[:, U:])
        nc.sync.dma_start(q_raw[:], query.rearrange("(p j) q -> p j q", j=PACK))
        for g in range(4):
            nc.sync.dma_start(
                kbytes[32 * g : 32 * g + 4, :].bitcast(I32), keys_scales[0, 4 * g : 4 * g + 4, :].bitcast(I32)
            )
        nc.sync.dma_start(high_sb[:, : PACK * U], high.rearrange("(p j) u -> p (j u)", j=PACK))
        nc.sync.dma_start(
            rows[0:PACK, :].rearrange("t (b r) -> t b r", r=RUN),
            vsc.rearrange("(b t r) o -> t b (r o)", t=PACK, r=RUN),
        )
        nc.sync.dma_start(
            rows[PACK : 2 * PACK, :].rearrange("t (b r) -> t b r", r=RUN),
            size.rearrange("o (b t r) -> (o t) b r", t=PACK, r=RUN),
        )
        for j in range(PACK):
            nc.sync.dma_start(vals_sb[j][:], vals_v[j])

        kg_words = tile([P, I], U16, "kg_words")
        kg_bytes = tile([P, I], U8, "kg_bytes")
        nc.vector.tensor_copy(kg_words[:], kwords[:].indirect(slots[:]))
        nc.vector.tensor_copy(kg_bytes[:], kbytes[:].indirect(slots[:]))

        turned = ps.tile([P, PACK, P], F32, name="turned")
        nc.tensor.transpose(turned[:, 0, :], rows[:], ident[:])
        cols = tile([P, 2 * PACK], F32, "cols")
        nc.scalar.copy(cols[:], turned[:, 0, : 2 * PACK])

        q_bf = tile([P, Q, PACK], BF16, "q_bf")
        nc.scalar.copy(
            q_bf[:].rearrange("p (c i) t -> p c t i", i=4), q_raw[:].rearrange("p t (c i) -> p c t i", i=4)
        )
        q_words = after("hi1", [P, Q], U32, "q_words")
        q_bytes = tile([P, Q], U8, "q_bytes")
        nc.vector.quantize_mx(q_words[:].bitcast(FP8X4), q_bytes[:], q_bf[:].rearrange("p q t -> p (q t)"))

        neg_max = after("val", [P, halves], F32, "neg_max")
        sums = after("hi2", [P, halves], F32, "sums")
        inv = tile([P, halves], F32, "inv")
        probs = []
        for h in range(halves):
            cs = slice(h * P, (h + 1) * P)
            score = ps.tile([P, I], F32, name="score%d" % h, tag="pair%d" % h)
            nc.tensor.matmul_mx(
                score[:], lhsT=q_words[:, cs].bitcast(FP8X4), lhsT_scale=q_bytes[:, cs],
                rhs=kg_words[:].bitcast(FP4X4), rhs_scale=kg_bytes[:], start=True, stop=True,
            )
            nc.vector.tensor_reduce(neg_max[:, h : h + 1], score[:], AXIS_X, ALU.max, negate=True)
            prob = tile([P, PACK, P], F32, "prob%d" % h)
            nc.scalar.activation(
                prob[:].rearrange("p t (b r) -> p t b r", r=RUN),
                score[:].rearrange("p (b t r) -> p t b r", t=PACK, r=RUN),
                ACT.Exp, bias=neg_max[:, h : h + 1], scale=1.0, accum_out=sums[:, h : h + 1],
            )
            probs.append(prob)
        nc.vector.reciprocal(inv[:], sums[:])
        w_banks = [ps.tile([P, 2, Q], F32, name="w_bank%d" % u) for u in range(2)]
        for h in range(halves):
            norm = tile([P, PACK, P], F32, "norm%d" % h)
            nc.scalar.activation(norm[:], probs[h][:], ACT.Copy, scale=inv[:, h : h + 1])
            for t in range(PACK):
                nc.tensor.transpose(w_banks[t // 2][:, t % 2, h * P : (h + 1) * P], norm[:, t, :], ident[:])
        w_planes = after("floor2", [P, PACK, Q], BF16, "w_planes")
        for t in range(PACK):
            nc.scalar.activation(
                w_planes[:, t, :], w_banks[t // 2][:, t % 2, :], ACT.Copy, scale=cols[:, PACK + t : PACK + t + 1]
            )
        w_bf = tile([P, Q, PACK], BF16, "w_bf")
        nc.scalar.copy(
            w_bf[:].rearrange("p (c i) t -> p c t i", i=4), w_planes[:].rearrange("p t (c i) -> p c t i", i=4)
        )
        w_words = tile([P, Q], U32, "w_words")
        w_bytes = tile([P, Q], U8, "w_bytes")
        nc.vector.quantize_mx(w_words[:].bitcast(FP8X4), w_bytes[:], w_bf[:].rearrange("p q t -> p (q t)"))

        out_banks = [ps.tile([P, PACK, P], F32, name="out_bank%d" % h) for h in range(halves)]
        y = tile([P, PACK, Q], F32, "y")
        out_v = out_0.rearrange("(p t) q -> p t q", t=PACK)

        for j in range(PACK):
            lo = after("lo%d" % min(j, 2), [P, I], F32, "lo%d" % j)
            hi = after("hi%d" % (j % 3), [P, I], F32, "hi%d" % j)
            val = after("val", [P, I], F32, "val%d" % j)
            low_window = low_first[:] if j == 0 else low_sb[:, (j - 1) * U : (j - 1) * U + WINDOW]
            nc.vector.tensor_copy(lo[:], low_window.indirect(classes[:]))
            nc.vector.tensor_copy(val[:], vals_sb[j][:].indirect(slots[:]))
            nc.vector.tensor_copy(hi[:], high_sb[:, j * U : j * U + WINDOW].indirect(classes[:]))
            floor = after("floor%d" % j, [P, I], F32, "floor%d" % j)
            cut = tile([P, PACK, P], F32, "cut%d" % j)
            for u in range(2):
                nc.vector.tensor_tensor(
                    floor[:, u * (I // 2) : (u + 1) * (I // 2)].rearrange("p (t b r) -> p t b r", t=2, r=RUN),
                    dealt(val)[:, 2 * u : 2 * u + 2], dealt(lo)[:, 2 * u : 2 * u + 2], ALU.max,
                )
            step = 1 if j == PACK - 1 else 2
            for t in range(0, PACK, step):
                nc.vector.tensor_tensor(
                    cut[:, t : t + step, :].rearrange("p t (b r) -> p t b r", r=RUN),
                    floor[:, t * P : (t + step) * P].rearrange("p (t b r) -> p t b r", t=step, r=RUN),
                    dealt(hi)[:, t : t + step], ALU.min,
                )
            v_bf = tile([P, P, PACK], BF16, "v_bf%d" % j)
            if j < PACK - 1:
                v_planes = after("floor3" if j == 2 else "v_planes%d" % j, [P, PACK, P], BF16, "v_planes%d" % j)
                for u in range(2):
                    bank = ps.tile([P, 2, P], F32, name="pair%d_%d" % (j, u), tag="pair%d" % u)
                    for t in range(2):
                        nc.tensor.transpose(bank[:, t, :], cut[:, 2 * u + t, :], ident[:])
                    for t in range(2):
                        place = 2 * u + t
                        nc.scalar.activation(
                            v_planes[:, place, :], bank[:, t, :], ACT.Copy, scale=cols[:, place : place + 1]
                        )
                nc.scalar.copy(
                    v_bf[:].rearrange("p (c i) t -> p c t i", i=4),
                    v_planes[:].rearrange("p t (c i) -> p c t i", i=4),
                )
            else:
                bank = ps.tile([P, PACK, P], F32, name="last_bank")
                for t in range(PACK):
                    nc.tensor.transpose(bank[:, t, :], cut[:, t, :], ident[:])
                for u in range(2):
                    es = slice(u * (P // 2), (u + 1) * (P // 2))
                    nc.vector.tensor_tensor(
                        v_bf[:, es, :], bank[:, :, es].rearrange("p t e -> p e t"),
                        cols[:, 0:PACK].unsqueeze(1).to_broadcast([P, P // 2, PACK]), ALU.mult,
                    )
            v_words = tile([P, P], U32, "v_words%d" % j)
            v_bytes = tile([P, P], U8, "v_bytes%d" % j)
            pieces = 2 if j == PACK - 1 else 1
            for u in range(pieces):
                es = slice(u * (P // pieces), (u + 1) * (P // pieces))
                nc.vector.quantize_mx(
                    v_words[:, es].bitcast(FP8X4), v_bytes[:, es], v_bf[:, es, :].rearrange("p e t -> p (e t)")
                )
            for h in range(halves):
                cs = slice(h * P, (h + 1) * P)
                nc.tensor.matmul_mx(
                    out_banks[h][:, j, :], lhsT=v_words[:].bitcast(FP8X4), lhsT_scale=v_bytes[:],
                    rhs=w_words[:, cs].bitcast(FP8X4), rhs_scale=w_bytes[:, cs], start=True, stop=True,
                )
            if j == 2:
                for h in range(halves):
                    nc.scalar.copy(y[:, 0:3, h * P : (h + 1) * P], out_banks[h][:, 0:3, :])
                nc.sync.dma_start(out_v[:, 0:3, :], y[:, 0:3, :])

        y_bf = [tile([P, P, PACK], BF16, "y_bf%d" % h) for h in range(halves)]
        for u in range(2):
            qs = slice(u * (P // 2), (u + 1) * (P // 2))
            nc.vector.tensor_copy(y_bf[0][:, qs, :], out_banks[0][:, :, qs].rearrange("p t q -> p q t"))
        nc.scalar.copy(y_bf[1][:], out_banks[1][:].rearrange("p t q -> p q t"))
        for h in (1, 0):
            nc.scalar.copy(y[:, 3, h * P : (h + 1) * P], out_banks[h][:, 3, :])
        y_words = tile([P, Q], U32, "y_words")
        y_bytes = tile([P, Q], U8, "y_bytes")
        for h, first, width in ((0, 0, P // 2), (0, P // 2, P // 2), (1, 0, P)):
            cs = slice(h * P + first, h * P + first + width)
            nc.vector.quantize_mx(
                y_words[:, cs].bitcast(FP8X4), y_bytes[:, cs],
                y_bf[h][:, first : first + width, :].rearrange("p q t -> p (q t)"),
            )
        nc.sync.dma_start(out_v[:, 3, :], y[:, 3, :])
        words_v = out_1[0].rearrange("p q t -> p (q t)").bitcast(I32)
        for h in range(halves):
            nc.sync.dma_start(words_v[:, h * P : (h + 1) * P], y_words[:, h * P : (h + 1) * P].bitcast(I32))
        for g in range(4):
            queue = nc.sync if g < 2 else nc.scalar
            queue.dma_start(out_2[0, 4 * g : 4 * g + 4, :].bitcast(I32), y_bytes[32 * g : 32 * g + 4, :].bitcast(I32))
